import numpy as np
import ml_dtypes


def mxq(x, axis, fmt="e4m3"):
    dtype, down = {"e4m3": (ml_dtypes.float8_e4m3fn, 7), "e5m2": (ml_dtypes.float8_e5m2, 14)}[fmt]
    v = np.moveaxis(np.asarray(x, np.float32).astype(ml_dtypes.bfloat16).astype(np.float64), axis, -1)
    blocks = v.reshape(v.shape[:-1] + (-1, 32))
    amax = np.abs(blocks).max(-1, keepdims=True)
    byte = np.maximum(np.where(amax > 0, np.frexp(amax)[1] - 1 + 127, 0) - down, 1)
    scale = np.exp2(byte - 127.0)
    codes = (blocks / scale).astype(np.float32).astype(dtype).astype(np.float64)
    return np.moveaxis((codes * scale).reshape(v.shape), -1, axis)


WIDE = False


def mx_kscale(k):
    if not WIDE:
        return np.ones(k)
    levels = np.array([10, -10, 5, -5, 0])
    if k % 512:
        return np.exp2(np.random.permutation(np.resize(levels, k // 32))).repeat(32)
    a = np.empty((k // 512, 16))
    for p in range(k // 512):
        a[p, :8] = np.random.permutation(np.resize(levels, 8))
        for g in range(8):
            far = levels[np.abs(levels - a[p, g]) >= 10]
            a[p, g + 8] = far[np.random.randint(len(far))]
    return np.exp2(a.ravel()).repeat(32)


BF16 = ml_dtypes.bfloat16


def bf(x):
    return np.asarray(x, np.float32).astype(BF16)


def f64(x):
    return np.asarray(x).astype(np.float64)


E2M1 = np.array([0.0, 0.5, 1.0, 1.5, 2.0, 3.0, 4.0, 6.0, -0.0, -0.5, -1.0, -1.5, -2.0, -3.0, -4.0, -6.0])


def pack_weight(w, fmt):
    k, n = w.shape
    w = f64(bf(w)).reshape(k // 32, 32, n)
    amax = np.abs(w).max(1)
    if fmt == "e4m3":
        byte = np.frexp(amax)[1] - 1 + 127 - 7
    else:
        mant, ex = np.frexp(amax / 6.0)
        byte = np.where(mant > 0.5, ex, ex - 1) + 127
    byte = np.clip(np.where(amax > 0, byte, 1), 1, 254)
    scaled = (w * np.exp2(127.0 - byte)[:, None, :]).reshape(k, n).astype(np.float32)
    by_word = np.ascontiguousarray(scaled.reshape(k // 512, 128, 4, n).transpose(0, 1, 3, 2))
    if fmt == "e4m3":
        words = by_word.astype(ml_dtypes.float8_e4m3fn).view(np.uint8)
    else:
        c = by_word.astype(ml_dtypes.float4_e2m1fn).view(np.uint8) & 0xF
        words = c[..., 0::2] | (c[..., 1::2] << 4)
    return np.ascontiguousarray(words), np.ascontiguousarray(byte.astype(np.uint8).reshape(k // 512, 16, n))


def unpack_weight(words, scales, fmt):
    g, p, n, _ = words.shape
    if fmt == "e4m3":
        vals = np.ascontiguousarray(words).view(ml_dtypes.float8_e4m3fn).astype(np.float64)
    else:
        nib = np.empty((g, p, n, 4), np.uint8)
        nib[..., 0::2] = words & 0xF
        nib[..., 1::2] = words >> 4
        vals = E2M1[nib]
    vals = vals * np.repeat(np.exp2(scales.astype(np.float64) - 127.0), 8, axis=1)[..., None]
    return vals.transpose(0, 1, 3, 2).reshape(g * 512, n)
def pack4(w):
    words, scales = pack_weight(w, "e2m1")
    return words.reshape(words.shape[0], 128, -1), scales


def unpack4(words, scales):
    return unpack_weight(words.reshape(words.shape[0], 128, -1, 2), scales, "e2m1")


M, D, T = 1024, 1024, 2048


def setup_inputs():
    s, t = mx_kscale(D), mx_kscale(D)
    w = np.random.standard_normal((D, T)) / s[:, None]
    early_words, early_scales = pack4(w)
    return {
        "q": bf(np.random.standard_normal((M, D)) / np.sqrt(D) / t),
        "early_words": early_words,
        "early_scales": early_scales,
        "early_gain": bf((1 + 0.1 * np.random.standard_normal(D)) * s * t),
        "mid_keys": bf(np.random.standard_normal((T, D))),
        "mid_gain": bf((1 + 0.1 * np.random.standard_normal(D)) * t),
        "temp": bf(1 + 0.1 * np.random.standard_normal(M)),
        "key_bias": bf(0.4 * np.random.standard_normal(T)),
    }


def reference(q, early_words, early_scales, early_gain, mid_keys, mid_gain, temp, key_bias):
    w = unpack4(early_words, early_scales)
    q_early = mxq(f64(q) * f64(early_gain), 1, "e4m3")
    from_early = q_early @ w
    q_plain = mxq(f64(q), 1, "e4m3")
    k_mid = mxq(f64(mid_keys) * f64(mid_gain), 1, "e4m3")
    from_mid = q_plain @ k_mid.T
    return (from_early + from_mid) * f64(temp)[:, None] + f64(key_bias)

@@ -1,0 +1,431 @@
+from contextlib import ExitStack
+
+import concourse.mybir as mybir
+from concourse.masks import make_identity
+
+M, D, T = 1024, 1024, 2048
+FLOPS = 2 * 2 * M * D * T
+
+F32 = mybir.dt.float32
+BF16 = mybir.dt.bfloat16
+I32 = mybir.dt.int32
+U32 = mybir.dt.uint32
+U8 = mybir.dt.uint8
+FP8X4 = mybir.dt.float8_e4m3fn_x4
+FP4X4 = mybir.dt.float4_e2m1fn_x4
+ALU = mybir.AluOpType
+ACT = mybir.ActivationFunctionType
+
+P = 128
+PASSES = 2
+Q_TILES = M // P
+ROWS = 256
+CHUNK = 512
+BANK = 512
+EARLY, PLAIN = 0, 1
+OUT_BUFS = 16
+
+
+def tile_cross_layer_key_scores_s1_kernel(
+    tc, q, early_words, early_scales, early_gain, mid_keys, mid_gain, temp, key_bias, out
+):
+    nc = tc.nc
+    q_rows = q.rearrange("(p j) k -> p j k", j=Q_TILES)
+    out_rows = out.rearrange("(p j) n -> p j n", j=Q_TILES)
+    w_words = early_words.bitcast(I32).rearrange("g p w -> p g w")
+    w_scale_rows = early_scales.bitcast(I32)
+
+    with ExitStack() as ctx:
+        keep = ctx.enter_context(tc.tile_pool(name="keep", bufs=1))
+        stage = ctx.enter_context(tc.tile_pool(name="stage", bufs=2))
+        psum = ctx.enter_context(tc.psum_pool(name="psum", bufs=1))
+        ctx.enter_context(tc.manual_schedule())
+
+        def kept(name, shape, dtype):
+            return keep.tile(shape, dtype, name=name, tag=name, align_bytes=64)
+
+        ident = kept("ident", [P, P], F32)
+        early_gain_sb = kept("early_gain_sb", [P, PASSES, 4], BF16)
+        mid_gain_sb = kept("mid_gain_sb", [P, PASSES, 4], BF16)
+        temp_bf = kept("temp_bf", [P, Q_TILES], BF16)
+        temp_sb = kept("temp_sb", [P, Q_TILES], F32)
+        bias_rows = kept("bias_rows", [P, T // P], BF16)
+        bias_all = kept("bias_all", [P, T], BF16)
+        w_scales = [kept("w_scales%d" % half, [P, T], U8) for half in range(2)]
+
+        q_raw, q_sorted, q_bf, q_codes, q_scales = {}, {}, {}, {}, {}
+        k_raw, k_sorted, k_bf, k_codes, k_scales = {}, {}, {}, {}, {}
+        w_codes, turned, sums, results = {}, {}, {}, {}
+        free_banks = list(range(8))
+
+        def take_bank():
+            b = free_banks.pop(0)
+            return b, psum.tile([P, BANK], F32, name="bank%d" % b, tag="bank%d" % b)
+
+        def setup():
+            make_identity(nc, ident[:])
+            for half in range(2):
+                nc.vector.memset(w_scales[half][:].bitcast(I32), 0)
+
+        def load_small():
+            nc.scalar.dma_start(out=temp_bf[:], in_=temp.rearrange("(p j) -> p j", j=Q_TILES))
+            nc.scalar.dma_start(out=bias_rows[:], in_=key_bias.rearrange("(p c) -> p c", p=P))
+            nc.scalar.dma_start(out=early_gain_sb[:], in_=early_gain.rearrange("(g p t) -> p g t", g=PASSES, t=4))
+
+        def load_mid_gain():
+            nc.sync.dma_start(out=mid_gain_sb[:], in_=mid_gain.rearrange("(g p t) -> p g t", g=PASSES, t=4))
+
+        def load_scales(half, queue):
+            plane = w_scales[half][:].bitcast(I32).rearrange("p (g w) -> p g w", g=PASSES)
+            words = T // 8
+            for quad in range(4):
+                queue.dma_start(
+                    out=plane[32 * quad : 32 * quad + 4],
+                    in_=w_scale_rows[:, 4 * quad : 4 * quad + 4, half * words : (half + 1) * words].rearrange(
+                        "g r w -> r g w"
+                    ),
+                )
+
+        def widen_temp():
+            nc.scalar.activation(out=temp_sb[:], in_=temp_bf[:], func=ACT.Copy)
+
+        def load_q(i):
+            q_raw[i] = kept("q_raw%d" % i, [P, 2 * D], BF16)
+            nc.sync.dma_start(
+                out=q_raw[i][:], in_=q_rows[:, 2 * i : 2 * i + 2, :].rearrange("p j k -> p (j k)")
+            )
+
+        def load_k(c, h):
+            k_raw[(c, h)] = kept("k_raw%d%d" % (c, h), [P, 2 * D], BF16)
+            first = c * CHUNK + h * ROWS
+            nc.sync.dma_start(
+                out=k_raw[(c, h)][:].rearrange("p (j k) -> p j k", j=2),
+                in_=mid_keys[first : first + ROWS, :].rearrange("(j p) k -> p j k", p=P),
+            )
+
+        def load_w(c, n=1):
+            words = CHUNK // 2
+            tile = kept("w_codes%d" % c, [P, PASSES, n * 2 * CHUNK], U8)
+            nc.sync.dma_start(out=tile[:].bitcast(I32), in_=w_words[:, :, c * words : (c + n) * words])
+            for x in range(n):
+                for g in range(PASSES):
+                    w_codes[(c + x, g)] = tile[:, g, x * 2 * CHUNK : (x + 1) * 2 * CHUNK]
+
+        def spread_bias():
+            words = bias_rows[:].bitcast(F32)
+            target = bias_all[:].bitcast(F32).rearrange("p (n c) -> p n c", c=8)
+            held = []
+            for half in range(2):
+                b, bank = take_bank()
+                held.append((b, bank))
+                for c in range(4):
+                    col = 4 * half + c
+                    nc.tensor.transpose(
+                        bank[:, c * P : (c + 1) * P], words[:, col : col + 1].to_broadcast([P, P]), ident[:]
+                    )
+            for half, (b, bank) in enumerate(held):
+                nc.scalar.copy(
+                    out=target[:, :, 4 * half : 4 * half + 4], in_=bank[:].rearrange("p (c n) -> p n c", c=4)
+                )
+                free_banks.append(b)
+
+        def sort_words(raw):
+            tile = stage.tile([P, D], F32, name="sorted_words", tag="sorted_words", bufs=3, align_bytes=64)
+            nc.scalar.copy(
+                out=tile[:].rearrange("p (a u w) -> p a u w", u=2, w=P),
+                in_=raw[:].bitcast(F32).rearrange("p (a w u) -> p a u w", u=2, w=P),
+            )
+            return tile
+
+        def sort_q(i):
+            q_sorted[i] = sort_words(q_raw[i])
+
+        def sort_k(c, h):
+            k_sorted[(c, h)] = sort_words(k_raw[(c, h)])
+
+        def turn(key, raw, in_order):
+            for g in range(PASSES):
+                b, bank = take_bank()
+                turned[key + (g,)] = (b, bank)
+                for u in range(2):
+                    for j in range(2):
+                        base = (j * PASSES + g) * 2 * P
+                        if in_order is None:
+                            words = raw[:].bitcast(F32)[:, base + u : base + 2 * P : 2]
+                        else:
+                            words = in_order[:, base + u * P : base + (u + 1) * P]
+                        col = u * ROWS + j * P
+                        nc.tensor.transpose(bank[:, col : col + P], words, ident[:])
+
+        def turn_q(i):
+            for kind in (EARLY, PLAIN):
+                q_bf[(i, kind)] = stage.tile(
+                    [P, PASSES * ROWS * 4], BF16, name="q_bf%d" % kind, tag="q_bf%d" % kind, align_bytes=64
+                )
+                q_codes[(i, kind)] = kept("q_codes%d%d" % (i, kind), [P, PASSES * ROWS], U32)
+                q_scales[(i, kind)] = kept("q_scales%d%d" % (i, kind), [P, PASSES * ROWS], U8)
+            turn(("q", i), q_raw[i], q_sorted.get(i))
+
+        def turn_k(c, h):
+            if h == 0:
+                for g in range(PASSES):
+                    k_bf[(c, g)] = stage.tile(
+                        [P, CHUNK * 4], BF16, name="k_bf%d" % g, tag="k_bf%d" % g, align_bytes=64
+                    )
+                    k_codes[(c, g)] = kept("k_codes%d%d" % (c, g), [P, CHUNK], U32)
+                    k_scales[(c, g)] = kept("k_scales%d%d" % (c, g), [P, CHUNK], U8)
+            turn(("k", c, h), k_raw[(c, h)], k_sorted.get((c, h)))
+
+        def gain_from_psum(target, bank, gain):
+            nc.vector.tensor_tensor(
+                out=target.rearrange("p (r u e) -> p r u e", u=2, e=2),
+                in0=bank[:].bitcast(BF16).rearrange("p (u r e) -> p r u e", u=2, e=2),
+                in1=gain.rearrange("p (u e) -> p u e", u=2).unsqueeze(1).to_broadcast([P, ROWS, 2, 2]),
+                op=ALU.mult,
+            )
+
+        def gain_q_from_psum(i, g):
+            width = ROWS * 4
+            gain_from_psum(
+                q_bf[(i, EARLY)][:, g * width : (g + 1) * width], turned[("q", i, g)][1], early_gain_sb[:, g, :]
+            )
+
+        def copy_q(i, g):
+            b, bank = turned[("q", i, g)]
+            width = ROWS * 2
+            nc.scalar.copy(
+                out=q_bf[(i, PLAIN)][:].bitcast(F32)[:, g * width : (g + 1) * width].rearrange(
+                    "p (r u) -> p r u", u=2
+                ),
+                in_=bank[:].rearrange("p (u r) -> p r u", u=2),
+            )
+            free_banks.append(b)
+
+        def gain_q(i):
+            nc.vector.tensor_tensor(
+                out=q_bf[(i, EARLY)][:].rearrange("p (g r t) -> p g r t", g=PASSES, t=4),
+                in0=q_bf[(i, PLAIN)][:].rearrange("p (g r t) -> p g r t", g=PASSES, t=4),
+                in1=early_gain_sb[:].unsqueeze(2).to_broadcast([P, PASSES, ROWS, 4]),
+                op=ALU.mult,
+            )
+
+        def quant_q(i, kind, gs=(0, 1)):
+            lo, hi = gs[0] * ROWS, (gs[-1] + 1) * ROWS
+            nc.vector.quantize_mx(
+                out=q_codes[(i, kind)][:, lo:hi].bitcast(FP8X4),
+                scales=q_scales[(i, kind)][:, lo:hi],
+                in_=q_bf[(i, kind)][:, 4 * lo : 4 * hi],
+            )
+
+        def gain_k(c, h, g):
+            b, bank = turned[("k", c, h, g)]
+            width = ROWS * 4
+            gain_from_psum(k_bf[(c, g)][:, h * width : (h + 1) * width], bank, mid_gain_sb[:, g, :])
+            free_banks.append(b)
+
+        def quant_k(c, g):
+            nc.vector.quantize_mx(
+                out=k_codes[(c, g)][:].bitcast(FP8X4), scales=k_scales[(c, g)][:], in_=k_bf[(c, g)][:]
+            )
+
+        def q_operand(m, kind, g):
+            cols = slice(g * ROWS + (m % 2) * P, g * ROWS + (m % 2 + 1) * P)
+            return q_codes[(m // 2, kind)][:, cols].bitcast(FP8X4), q_scales[(m // 2, kind)][:, cols]
+
+        def early(m, c):
+            sums[(m, c)] = take_bank()
+            for g in range(PASSES):
+                codes, scales = q_operand(m, EARLY, g)
+                nc.tensor.matmul_mx(
+                    out=sums[(m, c)][1][:],
+                    lhsT=codes,
+                    lhsT_scale=scales,
+                    rhs=w_codes[(c, g)].bitcast(FP4X4),
+                    rhs_scale=w_scales[c // 2][:, (2 * g + c % 2) * CHUNK : (2 * g + c % 2 + 1) * CHUNK],
+                    start=(g == 0),
+                    stop=False,
+                )
+
+        def mid(m, c):
+            for g in range(PASSES):
+                codes, scales = q_operand(m, PLAIN, g)
+                nc.tensor.matmul_mx(
+                    out=sums[(m, c)][1][:],
+                    lhsT=codes,
+                    lhsT_scale=scales,
+                    rhs=k_codes[(c, g)][:].bitcast(FP8X4),
+                    rhs_scale=k_scales[(c, g)][:],
+                    start=False,
+                    stop=(g == PASSES - 1),
+                )
+
+        def group(m, c):
+            early(m, c)
+            mid(m, c)
+
+        def new_result(m, c):
+            results[(m, c)] = stage.tile([P, CHUNK], F32, name="result", tag="result", bufs=OUT_BUFS)
+            return results[(m, c)]
+
+        def store(m, c):
+            nc.sync.dma_start(out=out_rows[:, m, c * CHUNK : (c + 1) * CHUNK], in_=results[(m, c)][:])
+
+        def finish(m, c):
+            b, bank = sums[(m, c)]
+            nc.vector.scalar_tensor_tensor(
+                out=new_result(m, c)[:],
+                in0=bank[:],
+                scalar=temp_sb[:, m : m + 1],
+                in1=bias_all[:, c * CHUNK : (c + 1) * CHUNK],
+                op0=ALU.mult,
+                op1=ALU.add,
+            )
+            free_banks.append(b)
+            store(m, c)
+
+        def park(m, c):
+            b, bank = sums[(m, c)]
+            nc.scalar.activation(out=new_result(m, c)[:], in_=bank[:], func=ACT.Copy, scale=temp_sb[:, m : m + 1])
+            free_banks.append(b)
+
+        def finish_parked(m, c):
+            result = results[(m, c)]
+            nc.vector.tensor_tensor(
+                out=result[:], in0=result[:], in1=bias_all[:, c * CHUNK : (c + 1) * CHUNK], op=ALU.add
+            )
+            store(m, c)
+
+        setup()
+        load_small()
+        load_q(0)
+        load_k(0, 0)
+        load_mid_gain()
+        load_w(0)
+        load_k(0, 1)
+        widen_temp()
+        load_scales(0, nc.scalar)
+        load_w(1)
+        load_q(1)
+        load_k(1, 0)
+        load_k(1, 1)
+        load_q(2)
+        load_q(3)
+        load_k(2, 0)
+        load_k(2, 1)
+        load_w(2, 2)
+        load_scales(1, nc.sync)
+        load_k(3, 0)
+        load_k(3, 1)
+        spread_bias()
+        turn_q(0)
+        for g in range(2):
+            gain_q_from_psum(0, g)
+            copy_q(0, g)
+        turn_k(0, 0)
+        quant_q(0, EARLY, (0,))
+        quant_q(0, EARLY, (1,))
+        sort_k(0, 1)
+        sort_q(1)
+        early(0, 0)
+        turn_k(0, 1)
+        early(1, 0)
+        gain_k(0, 0, 0)
+        gain_k(0, 0, 1)
+        quant_q(0, PLAIN)
+        gain_k(0, 1, 0)
+        gain_k(0, 1, 1)
+        turn_q(1)
+        copy_q(1, 0)
+        copy_q(1, 1)
+        early(0, 1)
+        early(1, 1)
+        quant_k(0, 0)
+        quant_k(0, 1)
+        sort_k(1, 0)
+        sort_k(1, 1)
+        mid(0, 0)
+        mid(1, 0)
+        gain_q(1)
+        turn_k(1, 0)
+        park(0, 0)
+        park(1, 0)
+        quant_q(1, PLAIN)
+        quant_q(1, EARLY)
+        gain_k(1, 0, 0)
+        gain_k(1, 0, 1)
+        turn_k(1, 1)
+        group(2, 0)
+        gain_k(1, 1, 0)
+        gain_k(1, 1, 1)
+        sort_q(2)
+        group(3, 0)
+        park(2, 0)
+        turn_q(2)
+        park(3, 0)
+        quant_k(1, 0)
+        quant_k(1, 1)
+        copy_q(2, 0)
+        copy_q(2, 1)
+        early(2, 1)
+        early(3, 1)
+        sort_q(3)
+        mid(0, 1)
+        mid(1, 1)
+        gain_q(2)
+        turn_q(3)
+        park(0, 1)
+        park(1, 1)
+        quant_q(2, PLAIN)
+        quant_q(2, EARLY)
+        mid(2, 1)
+        mid(3, 1)
+        copy_q(3, 0)
+        copy_q(3, 1)
+        sort_k(2, 0)
+        sort_k(2, 1)
+        finish(2, 1)
+        group(4, 0)
+        finish(3, 1)
+        gain_q(3)
+        group(5, 0)
+        turn_k(2, 0)
+        turn_k(2, 1)
+        quant_q(3, PLAIN)
+        quant_q(3, EARLY)
+        finish(4, 0)
+        group(4, 1)
+        finish(5, 0)
+        group(5, 1)
+        gain_k(2, 0, 0)
+        gain_k(2, 0, 1)
+        finish(4, 1)
+        group(6, 0)
+        gain_k(2, 1, 0)
+        gain_k(2, 1, 1)
+        finish(5, 1)
+        sort_k(3, 0)
+        sort_k(3, 1)
+        group(7, 0)
+        quant_k(2, 0)
+        quant_k(2, 1)
+        finish(6, 0)
+        group(6, 1)
+        finish(7, 0)
+        group(7, 1)
+        turn_k(3, 0)
+        turn_k(3, 1)
+        finish(6, 1)
+        parked = [(0, 0), (1, 0), (2, 0), (3, 0), (0, 1), (1, 1)]
+        extra = [
+            lambda: gain_k(3, 0, 0), lambda: gain_k(3, 0, 1), lambda: gain_k(3, 1, 0), lambda: gain_k(3, 1, 1),
+            lambda: quant_k(3, 0), lambda: quant_k(3, 1),
+        ] + [(lambda mc=mc: finish_parked(*mc)) for mc in parked]
+        prev = (7, 1)
+        for c in (2, 3):
+            for m in range(8):
+                group(m, c)
+                finish(*prev)
+                if extra:
+                    extra.pop(0)()
+                prev = (m, c)
+        finish(*prev)

@@ -23,7 +23,8 @@ ROWS = 256
 CHUNK = 512
 BANK = 512
 EARLY, PLAIN = 0, 1
-OUT_BUFS = 16
+OUT_BUFS = 20
+WARM_PASSES = 12
 
 
 def tile_cross_layer_key_scores_s1_kernel(
@@ -42,7 +43,7 @@ def tile_cross_layer_key_scores_s1_kernel(
         ctx.enter_context(tc.manual_schedule())
 
         def kept(name, shape, dtype):
-            return keep.tile(shape, dtype, name=name, tag=name, align_bytes=64)
+            return keep.tile(shape, dtype, name=name, tag=name, align_bytes=256)
 
         ident = kept("ident", [P, P], F32)
         early_gain_sb = kept("early_gain_sb", [P, PASSES, 4], BF16)
@@ -55,7 +56,7 @@ def tile_cross_layer_key_scores_s1_kernel(
 
         q_raw, q_sorted, q_bf, q_codes, q_scales = {}, {}, {}, {}, {}
         k_raw, k_sorted, k_bf, k_codes, k_scales = {}, {}, {}, {}, {}
-        w_codes, turned, sums, results = {}, {}, {}, {}
+        w_codes, turned, sums, results, first_raw = {}, {}, {}, {}, {}
         free_banks = list(range(8))
 
         def take_bank():
@@ -64,16 +65,42 @@ def tile_cross_layer_key_scores_s1_kernel(
 
         def setup():
             make_identity(nc, ident[:])
-            for half in range(2):
-                nc.vector.memset(w_scales[half][:].bitcast(I32), 0)
+
+        def clear_scales(half):
+            nc.vector.memset(w_scales[half][:].bitcast(I32), 0)
+
+        def warm_up():
+            zeros = kept("zeros", [P, 4 * P], BF16)
+            codes = kept("zero_codes", [P, P], U32)
+            scales = kept("zero_scales", [P, P], U8)
+            nc.vector.memset(zeros[:], 0.0)
+            nc.vector.quantize_mx(out=codes[:].bitcast(FP8X4), scales=scales[:], in_=zeros[:])
+            b, bank = take_bank()
+            for n in range(WARM_PASSES):
+                nc.tensor.matmul_mx(
+                    out=bank[:, (n % 4) * P : (n % 4 + 1) * P],
+                    lhsT=codes[:].bitcast(FP8X4),
+                    lhsT_scale=scales[:],
+                    rhs=codes[:].bitcast(FP8X4),
+                    rhs_scale=scales[:],
+                    start=True,
+                    stop=True,
+                )
+            free_banks.append(b)
 
         def load_small():
-            nc.scalar.dma_start(out=temp_bf[:], in_=temp.rearrange("(p j) -> p j", j=Q_TILES))
-            nc.scalar.dma_start(out=bias_rows[:], in_=key_bias.rearrange("(p c) -> p c", p=P))
+            nc.gpsimd.dma_start(out=bias_rows[:], in_=key_bias.rearrange("(p c) -> p c", p=P))
+
+        def load_early_gain():
             nc.scalar.dma_start(out=early_gain_sb[:], in_=early_gain.rearrange("(g p t) -> p g t", g=PASSES, t=4))
+            nc.scalar.dma_start(out=temp_bf[:], in_=temp.rearrange("(p j) -> p j", j=Q_TILES))
+
+        def load_first(j):
+            first_raw[j] = kept("first_raw%d" % j, [P, D], BF16)
+            nc.sync.dma_start(out=first_raw[j][:], in_=q_rows[:, j, :])
 
         def load_mid_gain():
-            nc.sync.dma_start(out=mid_gain_sb[:], in_=mid_gain.rearrange("(g p t) -> p g t", g=PASSES, t=4))
+            nc.scalar.dma_start(out=mid_gain_sb[:], in_=mid_gain.rearrange("(g p t) -> p g t", g=PASSES, t=4))
 
         def load_scales(half, queue):
             plane = w_scales[half][:].bitcast(I32).rearrange("p (g w) -> p g w", g=PASSES)
@@ -130,7 +157,7 @@ def tile_cross_layer_key_scores_s1_kernel(
                 free_banks.append(b)
 
         def sort_words(raw):
-            tile = stage.tile([P, D], F32, name="sorted_words", tag="sorted_words", bufs=3, align_bytes=64)
+            tile = stage.tile([P, D], F32, name="sorted_words", tag="sorted_words", bufs=3, align_bytes=256)
             nc.scalar.copy(
                 out=tile[:].rearrange("p (a u w) -> p a u w", u=2, w=P),
                 in_=raw[:].bitcast(F32).rearrange("p (a w u) -> p a u w", u=2, w=P),
@@ -157,37 +184,79 @@ def tile_cross_layer_key_scores_s1_kernel(
                         col = u * ROWS + j * P
                         nc.tensor.transpose(bank[:, col : col + P], words, ident[:])
 
-        def turn_q(i):
+        def new_q(i):
             for kind in (EARLY, PLAIN):
                 q_bf[(i, kind)] = stage.tile(
-                    [P, PASSES * ROWS * 4], BF16, name="q_bf%d" % kind, tag="q_bf%d" % kind, align_bytes=64
+                    [P, PASSES * ROWS * 4], BF16, name="q_bf%d" % kind, tag="q_bf%d" % kind, align_bytes=256
                 )
                 q_codes[(i, kind)] = kept("q_codes%d%d" % (i, kind), [P, PASSES * ROWS], U32)
                 q_scales[(i, kind)] = kept("q_scales%d%d" % (i, kind), [P, PASSES * ROWS], U8)
+
+        def turn_q(i):
+            new_q(i)
             turn(("q", i), q_raw[i], q_sorted.get(i))
+
+        def turn_first(j):
+            if j == 0:
+                new_q(0)
+            b, bank = take_bank()
+            turned[("first", j)] = (b, bank)
+            words = first_raw[j][:].bitcast(F32)
+            for g in range(PASSES):
+                for u in range(2):
+                    col = (2 * g + u) * P
+                    nc.tensor.transpose(bank[:, col : col + P], words[:, 2 * g * P + u : 2 * (g + 1) * P : 2], ident[:])
+
+        def gain_first(j, g):
+            lo = (g * ROWS + j * P) * 4
+            gain_from_psum(
+                q_bf[(0, EARLY)][:, lo : lo + 4 * P],
+                turned[("first", j)][1][:, 2 * g * P : 2 * (g + 1) * P],
+                early_gain_sb[:, g, :],
+                P,
+            )
+
+        def quant_first(j, g):
+            lo = g * ROWS + j * P
+            nc.vector.quantize_mx(
+                out=q_codes[(0, EARLY)][:, lo : lo + P].bitcast(FP8X4),
+                scales=q_scales[(0, EARLY)][:, lo : lo + P],
+                in_=q_bf[(0, EARLY)][:, 4 * lo : 4 * (lo + P)],
+            )
+
+        def copy_first(j):
+            b, bank = turned[("first", j)]
+            nc.scalar.copy(
+                out=q_bf[(0, PLAIN)][:].bitcast(F32).rearrange("p (g j r u) -> p g j r u", g=PASSES, j=2, u=2)[:, :, j],
+                in_=bank[:].rearrange("p (g u r) -> p g r u", g=PASSES, u=2),
+            )
+            free_banks.append(b)
 
         def turn_k(c, h):
             if h == 0:
                 for g in range(PASSES):
                     k_bf[(c, g)] = stage.tile(
-                        [P, CHUNK * 4], BF16, name="k_bf%d" % g, tag="k_bf%d" % g, align_bytes=64
+                        [P, CHUNK * 4], BF16, name="k_bf%d" % g, tag="k_bf%d" % g, align_bytes=256
                     )
                     k_codes[(c, g)] = kept("k_codes%d%d" % (c, g), [P, CHUNK], U32)
                     k_scales[(c, g)] = kept("k_scales%d%d" % (c, g), [P, CHUNK], U8)
             turn(("k", c, h), k_raw[(c, h)], k_sorted.get((c, h)))
 
-        def gain_from_psum(target, bank, gain):
+        def gain_from_psum(target, words, gain, rows):
             nc.vector.tensor_tensor(
                 out=target.rearrange("p (r u e) -> p r u e", u=2, e=2),
-                in0=bank[:].bitcast(BF16).rearrange("p (u r e) -> p r u e", u=2, e=2),
-                in1=gain.rearrange("p (u e) -> p u e", u=2).unsqueeze(1).to_broadcast([P, ROWS, 2, 2]),
+                in0=words.bitcast(BF16).rearrange("p (u r e) -> p r u e", u=2, e=2),
+                in1=gain.rearrange("p (u e) -> p u e", u=2).unsqueeze(1).to_broadcast([P, rows, 2, 2]),
                 op=ALU.mult,
             )
 
         def gain_q_from_psum(i, g):
             width = ROWS * 4
             gain_from_psum(
-                q_bf[(i, EARLY)][:, g * width : (g + 1) * width], turned[("q", i, g)][1], early_gain_sb[:, g, :]
+                q_bf[(i, EARLY)][:, g * width : (g + 1) * width],
+                turned[("q", i, g)][1][:],
+                early_gain_sb[:, g, :],
+                ROWS,
             )
 
         def copy_q(i, g):
@@ -220,7 +289,7 @@ def tile_cross_layer_key_scores_s1_kernel(
         def gain_k(c, h, g):
             b, bank = turned[("k", c, h, g)]
             width = ROWS * 4
-            gain_from_psum(k_bf[(c, g)][:, h * width : (h + 1) * width], bank, mid_gain_sb[:, g, :])
+            gain_from_psum(k_bf[(c, g)][:, h * width : (h + 1) * width], bank[:], mid_gain_sb[:, g, :], ROWS)
             free_banks.append(b)
 
         def quant_k(c, g):
@@ -263,6 +332,51 @@ def tile_cross_layer_key_scores_s1_kernel(
             early(m, c)
             mid(m, c)
 
+        def narrow_group(m, c, part):
+            b, bank = take_bank()
+            sums[(m, c, part)] = (b, bank)
+            lo = part * P
+            for g in range(PASSES):
+                codes, scales = q_operand(m, EARLY, g)
+                base = (2 * g + c % 2) * CHUNK + lo
+                nc.tensor.matmul_mx(
+                    out=bank[:, :P],
+                    lhsT=codes,
+                    lhsT_scale=scales,
+                    rhs=w_codes[(c, g)][:, 2 * lo : 2 * (lo + P)].bitcast(FP4X4),
+                    rhs_scale=w_scales[c // 2][:, base : base + P],
+                    start=(g == 0),
+                    stop=False,
+                )
+            for g in range(PASSES):
+                codes, scales = q_operand(m, PLAIN, g)
+                nc.tensor.matmul_mx(
+                    out=bank[:, :P],
+                    lhsT=codes,
+                    lhsT_scale=scales,
+                    rhs=k_codes[(c, g)][:, lo : lo + P].bitcast(FP8X4),
+                    rhs_scale=k_scales[(c, g)][:, lo : lo + P],
+                    start=False,
+                    stop=(g == PASSES - 1),
+                )
+
+        def narrow_finish(m, c, part):
+            b, bank = sums[(m, c, part)]
+            if part % 2 == 0:
+                results[(m, c)] = stage.tile([P, 2 * P], F32, name="narrow_result", tag="narrow_result")
+            first = c * CHUNK + part * P
+            nc.vector.scalar_tensor_tensor(
+                out=results[(m, c)][:, (part % 2) * P : (part % 2 + 1) * P],
+                in0=bank[:, :P],
+                scalar=temp_sb[:, m : m + 1],
+                in1=bias_all[:, first : first + P],
+                op0=ALU.mult,
+                op1=ALU.add,
+            )
+            free_banks.append(b)
+            if part % 2 == 1:
+                nc.sync.dma_start(out=out_rows[:, m, first - P : first + P], in_=results[(m, c)][:])
+
         def new_result(m, c):
             results[(m, c)] = stage.tile([P, CHUNK], F32, name="result", tag="result", bufs=OUT_BUFS)
             return results[(m, c)]
@@ -288,22 +402,26 @@ def tile_cross_layer_key_scores_s1_kernel(
             nc.scalar.activation(out=new_result(m, c)[:], in_=bank[:], func=ACT.Copy, scale=temp_sb[:, m : m + 1])
             free_banks.append(b)
 
-        def finish_parked(m, c):
+        def finish_parked(m, c, engine):
             result = results[(m, c)]
-            nc.vector.tensor_tensor(
+            engine.tensor_tensor(
                 out=result[:], in0=result[:], in1=bias_all[:, c * CHUNK : (c + 1) * CHUNK], op=ALU.add
             )
             store(m, c)
 
         setup()
         load_small()
+        load_early_gain()
         load_q(0)
         load_k(0, 0)
-        load_mid_gain()
         load_w(0)
-        load_k(0, 1)
-        widen_temp()
+        clear_scales(0)
         load_scales(0, nc.scalar)
+        warm_up()
+        clear_scales(1)
+        load_mid_gain()
+        widen_temp()
+        load_k(0, 1)
         load_w(1)
         load_q(1)
         load_k(1, 0)
@@ -316,116 +434,124 @@ def tile_cross_layer_key_scores_s1_kernel(
         load_scales(1, nc.sync)
         load_k(3, 0)
         load_k(3, 1)
-        spread_bias()
         turn_q(0)
+        turn_k(0, 0)
         for g in range(2):
             gain_q_from_psum(0, g)
             copy_q(0, g)
-        turn_k(0, 0)
+        spread_bias()
         quant_q(0, EARLY, (0,))
         quant_q(0, EARLY, (1,))
-        sort_k(0, 1)
-        sort_q(1)
         early(0, 0)
-        turn_k(0, 1)
         early(1, 0)
         gain_k(0, 0, 0)
         gain_k(0, 0, 1)
-        quant_q(0, PLAIN)
-        gain_k(0, 1, 0)
-        gain_k(0, 1, 1)
+        turn_k(0, 1)
         turn_q(1)
+        quant_q(0, PLAIN)
         copy_q(1, 0)
         copy_q(1, 1)
+        gain_k(0, 1, 0)
+        gain_k(0, 1, 1)
         early(0, 1)
         early(1, 1)
-        quant_k(0, 0)
-        quant_k(0, 1)
         sort_k(1, 0)
         sort_k(1, 1)
+        quant_k(0, 0)
+        quant_k(0, 1)
         mid(0, 0)
         mid(1, 0)
         gain_q(1)
         turn_k(1, 0)
+        turn_k(1, 1)
         park(0, 0)
         park(1, 0)
         quant_q(1, PLAIN)
         quant_q(1, EARLY)
         gain_k(1, 0, 0)
         gain_k(1, 0, 1)
-        turn_k(1, 1)
         group(2, 0)
         gain_k(1, 1, 0)
         gain_k(1, 1, 1)
         sort_q(2)
+        sort_q(3)
         group(3, 0)
-        park(2, 0)
-        turn_q(2)
-        park(3, 0)
         quant_k(1, 0)
         quant_k(1, 1)
+        turn_q(2)
+        finish(2, 0)
+        turn_q(3)
         copy_q(2, 0)
         copy_q(2, 1)
-        early(2, 1)
-        early(3, 1)
-        sort_q(3)
+        finish(3, 0)
+        copy_q(3, 0)
+        copy_q(3, 1)
         mid(0, 1)
         mid(1, 1)
         gain_q(2)
-        turn_q(3)
-        park(0, 1)
-        park(1, 1)
+        group(2, 1)
         quant_q(2, PLAIN)
         quant_q(2, EARLY)
-        mid(2, 1)
-        mid(3, 1)
-        copy_q(3, 0)
-        copy_q(3, 1)
+        park(0, 1)
+        park(1, 1)
         sort_k(2, 0)
         sort_k(2, 1)
-        finish(2, 1)
-        group(4, 0)
-        finish(3, 1)
+        group(3, 1)
         gain_q(3)
-        group(5, 0)
-        turn_k(2, 0)
-        turn_k(2, 1)
+        park(2, 1)
+        group(4, 0)
         quant_q(3, PLAIN)
         quant_q(3, EARLY)
-        finish(4, 0)
+        park(3, 1)
+        group(5, 0)
+        park(4, 0)
+        turn_k(2, 0)
+        turn_k(2, 1)
+        park(5, 0)
         group(4, 1)
-        finish(5, 0)
-        group(5, 1)
         gain_k(2, 0, 0)
         gain_k(2, 0, 1)
-        finish(4, 1)
-        group(6, 0)
         gain_k(2, 1, 0)
         gain_k(2, 1, 1)
-        finish(5, 1)
+        group(5, 1)
         sort_k(3, 0)
         sort_k(3, 1)
-        group(7, 0)
+        park(4, 1)
+        group(6, 0)
         quant_k(2, 0)
         quant_k(2, 1)
-        finish(6, 0)
-        group(6, 1)
-        finish(7, 0)
-        group(7, 1)
+        finish(5, 1)
+        group(7, 0)
+        park(6, 0)
         turn_k(3, 0)
         turn_k(3, 1)
+        finish(7, 0)
+        group(6, 1)
+        gain_k(3, 0, 0)
+        gain_k(3, 0, 1)
+        group(7, 1)
         finish(6, 1)
-        parked = [(0, 0), (1, 0), (2, 0), (3, 0), (0, 1), (1, 1)]
+        parked = [(6, 0), (0, 0), (1, 0), (0, 1), (1, 1), (2, 1), (3, 1), (4, 0), (5, 0), (4, 1)]
         extra = [
-            lambda: gain_k(3, 0, 0), lambda: gain_k(3, 0, 1), lambda: gain_k(3, 1, 0), lambda: gain_k(3, 1, 1),
+            lambda: gain_k(3, 1, 0), lambda: gain_k(3, 1, 1),
             lambda: quant_k(3, 0), lambda: quant_k(3, 1),
-        ] + [(lambda mc=mc: finish_parked(*mc)) for mc in parked]
+        ]
+        finish_parked(*parked.pop(0), nc.gpsimd)
+        finish_parked(*parked.pop(0), nc.gpsimd)
         prev = (7, 1)
         for c in (2, 3):
             for m in range(8):
-                group(m, c)
-                finish(*prev)
-                if extra:
-                    extra.pop(0)()
-                prev = (m, c)
+                if (m, c) != (7, 3):
+                    group(m, c)
+                    finish(*prev)
+                    if extra:
+                        extra.pop(0)()
+                    if parked:
+                        finish_parked(*parked.pop(0), nc.gpsimd)
+                    prev = (m, c)
+        narrow_group(7, 3, 0)
         finish(*prev)
+        for part in range(1, 4):
+            narrow_group(7, 3, part)
+            narrow_finish(7, 3, part - 1)
+        narrow_finish(7, 3, 3)

@@ -24,7 +24,6 @@ CHUNK = 512
 BANK = 512
 EARLY, PLAIN = 0, 1
 OUT_BUFS = 20
-WARM_PASSES = 12
 
 
 def tile_cross_layer_key_scores_s1_kernel(
@@ -50,8 +49,9 @@ def tile_cross_layer_key_scores_s1_kernel(
         mid_gain_sb = kept("mid_gain_sb", [P, PASSES, 4], BF16)
         temp_bf = kept("temp_bf", [P, Q_TILES], BF16)
         temp_sb = kept("temp_sb", [P, Q_TILES], F32)
-        bias_rows = kept("bias_rows", [P, T // P], BF16)
-        bias_all = kept("bias_all", [P, T], BF16)
+        bias_all = [kept("bias_all%d" % half, [P, T // 2], BF16) for half in range(2)]
+        zero_codes = kept("zero_codes", [P, P], U32)
+        zero_scales = kept("zero_scales", [P, P], U8)
         w_scales = [kept("w_scales%d" % half, [P, T], U8) for half in range(2)]
 
         q_raw, q_sorted, q_bf, q_codes, q_scales = {}, {}, {}, {}, {}
@@ -69,27 +69,28 @@ def tile_cross_layer_key_scores_s1_kernel(
         def clear_scales(half):
             nc.vector.memset(w_scales[half][:].bitcast(I32), 0)
 
-        def warm_up():
+        def make_zeros():
             zeros = kept("zeros", [P, 4 * P], BF16)
-            codes = kept("zero_codes", [P, P], U32)
-            scales = kept("zero_scales", [P, P], U8)
             nc.vector.memset(zeros[:], 0.0)
-            nc.vector.quantize_mx(out=codes[:].bitcast(FP8X4), scales=scales[:], in_=zeros[:])
+            nc.vector.quantize_mx(out=zero_codes[:].bitcast(FP8X4), scales=zero_scales[:], in_=zeros[:])
+
+        def warm_up(passes):
             b, bank = take_bank()
-            for n in range(WARM_PASSES):
+            for n in range(passes):
                 nc.tensor.matmul_mx(
                     out=bank[:, (n % 4) * P : (n % 4 + 1) * P],
-                    lhsT=codes[:].bitcast(FP8X4),
-                    lhsT_scale=scales[:],
-                    rhs=codes[:].bitcast(FP8X4),
-                    rhs_scale=scales[:],
+                    lhsT=zero_codes[:].bitcast(FP8X4),
+                    lhsT_scale=zero_scales[:],
+                    rhs=zero_codes[:].bitcast(FP8X4),
+                    rhs_scale=zero_scales[:],
                     start=True,
                     stop=True,
                 )
             free_banks.append(b)
 
-        def load_small():
-            nc.gpsimd.dma_start(out=bias_rows[:], in_=key_bias.rearrange("(p c) -> p c", p=P))
+        def load_bias(half):
+            cols = slice(half * T // 2, (half + 1) * T // 2)
+            nc.sync.dma_start(out=bias_all[half][:], in_=key_bias[cols].partition_broadcast(P))
 
         def load_early_gain():
             nc.scalar.dma_start(out=early_gain_sb[:], in_=early_gain.rearrange("(g p t) -> p g t", g=PASSES, t=4))
@@ -137,24 +138,6 @@ def tile_cross_layer_key_scores_s1_kernel(
             for x in range(n):
                 for g in range(PASSES):
                     w_codes[(c + x, g)] = tile[:, g, x * 2 * CHUNK : (x + 1) * 2 * CHUNK]
-
-        def spread_bias():
-            words = bias_rows[:].bitcast(F32)
-            target = bias_all[:].bitcast(F32).rearrange("p (n c) -> p n c", c=8)
-            held = []
-            for half in range(2):
-                b, bank = take_bank()
-                held.append((b, bank))
-                for c in range(4):
-                    col = 4 * half + c
-                    nc.tensor.transpose(
-                        bank[:, c * P : (c + 1) * P], words[:, col : col + 1].to_broadcast([P, P]), ident[:]
-                    )
-            for half, (b, bank) in enumerate(held):
-                nc.scalar.copy(
-                    out=target[:, :, 4 * half : 4 * half + 4], in_=bank[:].rearrange("p (c n) -> p n c", c=4)
-                )
-                free_banks.append(b)
 
         def sort_words(raw):
             tile = stage.tile([P, D], F32, name="sorted_words", tag="sorted_words", bufs=3, align_bytes=256)
@@ -369,7 +352,7 @@ def tile_cross_layer_key_scores_s1_kernel(
                 out=results[(m, c)][:, (part % 2) * P : (part % 2 + 1) * P],
                 in0=bank[:, :P],
                 scalar=temp_sb[:, m : m + 1],
-                in1=bias_all[:, first : first + P],
+                in1=bias_all[c // 2][:, first % (T // 2) : first % (T // 2) + P],
                 op0=ALU.mult,
                 op1=ALU.add,
             )
@@ -390,7 +373,7 @@ def tile_cross_layer_key_scores_s1_kernel(
                 out=new_result(m, c)[:],
                 in0=bank[:],
                 scalar=temp_sb[:, m : m + 1],
-                in1=bias_all[:, c * CHUNK : (c + 1) * CHUNK],
+                in1=bias_all[c // 2][:, (c % 2) * CHUNK : (c % 2 + 1) * CHUNK],
                 op0=ALU.mult,
                 op1=ALU.add,
             )
@@ -405,19 +388,18 @@ def tile_cross_layer_key_scores_s1_kernel(
         def finish_parked(m, c, engine):
             result = results[(m, c)]
             engine.tensor_tensor(
-                out=result[:], in0=result[:], in1=bias_all[:, c * CHUNK : (c + 1) * CHUNK], op=ALU.add
+                out=result[:], in0=result[:], in1=bias_all[c // 2][:, (c % 2) * CHUNK : (c % 2 + 1) * CHUNK], op=ALU.add
             )
             store(m, c)
 
         setup()
-        load_small()
         load_early_gain()
         load_q(0)
         load_k(0, 0)
         load_w(0)
+        make_zeros()
         clear_scales(0)
         load_scales(0, nc.scalar)
-        warm_up()
         clear_scales(1)
         load_mid_gain()
         widen_temp()
@@ -428,41 +410,46 @@ def tile_cross_layer_key_scores_s1_kernel(
         load_k(1, 1)
         load_q(2)
         load_q(3)
+        load_bias(0)
         load_k(2, 0)
         load_k(2, 1)
         load_w(2, 2)
         load_scales(1, nc.sync)
         load_k(3, 0)
         load_k(3, 1)
+        load_bias(1)
+        warm_up(22)
         turn_q(0)
+        warm_up(10)
         turn_k(0, 0)
         for g in range(2):
             gain_q_from_psum(0, g)
             copy_q(0, g)
-        spread_bias()
         quant_q(0, EARLY, (0,))
         quant_q(0, EARLY, (1,))
+        sort_k(0, 1)
+        sort_q(1)
         early(0, 0)
         early(1, 0)
         gain_k(0, 0, 0)
         gain_k(0, 0, 1)
         turn_k(0, 1)
-        turn_q(1)
         quant_q(0, PLAIN)
-        copy_q(1, 0)
-        copy_q(1, 1)
+        early(0, 1)
+        turn_q(1)
         gain_k(0, 1, 0)
         gain_k(0, 1, 1)
-        early(0, 1)
+        copy_q(1, 0)
+        copy_q(1, 1)
         early(1, 1)
-        sort_k(1, 0)
         sort_k(1, 1)
+        turn_k(1, 0)
         quant_k(0, 0)
         quant_k(0, 1)
+        sort_q(2)
         mid(0, 0)
         mid(1, 0)
         gain_q(1)
-        turn_k(1, 0)
         turn_k(1, 1)
         park(0, 0)
         park(1, 0)
@@ -473,7 +460,6 @@ def tile_cross_layer_key_scores_s1_kernel(
         group(2, 0)
         gain_k(1, 1, 0)
         gain_k(1, 1, 1)
-        sort_q(2)
         sort_q(3)
         group(3, 0)
         quant_k(1, 0)
@@ -503,6 +489,8 @@ def tile_cross_layer_key_scores_s1_kernel(
         quant_q(3, PLAIN)
         quant_q(3, EARLY)
         park(3, 1)
+        finish_parked(2, 1, nc.gpsimd)
+        finish_parked(3, 1, nc.gpsimd)
         group(5, 0)
         park(4, 0)
         turn_k(2, 0)
@@ -516,7 +504,7 @@ def tile_cross_layer_key_scores_s1_kernel(
         group(5, 1)
         sort_k(3, 0)
         sort_k(3, 1)
-        park(4, 1)
+        finish(4, 1)
         group(6, 0)
         quant_k(2, 0)
         quant_k(2, 1)
@@ -531,7 +519,7 @@ def tile_cross_layer_key_scores_s1_kernel(
         gain_k(3, 0, 1)
         group(7, 1)
         finish(6, 1)
-        parked = [(6, 0), (0, 0), (1, 0), (0, 1), (1, 1), (2, 1), (3, 1), (4, 0), (5, 0), (4, 1)]
+        parked = [(6, 0), (0, 0), (1, 0), (0, 1), (1, 1), (4, 0), (5, 0)]
         extra = [
             lambda: gain_k(3, 1, 0), lambda: gain_k(3, 1, 1),
             lambda: quant_k(3, 0), lambda: quant_k(3, 1),

@@ -179,41 +179,20 @@ def tile_cross_layer_key_scores_s1_kernel(
             new_q(i)
             turn(("q", i), q_raw[i], q_sorted.get(i))
 
-        def turn_first(j):
-            if j == 0:
-                new_q(0)
-            b, bank = take_bank()
-            turned[("first", j)] = (b, bank)
-            words = first_raw[j][:].bitcast(F32)
+        def turn_first():
+            new_q(0)
             for g in range(PASSES):
-                for u in range(2):
-                    col = (2 * g + u) * P
-                    nc.tensor.transpose(bank[:, col : col + P], words[:, 2 * g * P + u : 2 * (g + 1) * P : 2], ident[:])
-
-        def gain_first(j, g):
-            lo = (g * ROWS + j * P) * 4
-            gain_from_psum(
-                q_bf[(0, EARLY)][:, lo : lo + 4 * P],
-                turned[("first", j)][1][:, 2 * g * P : 2 * (g + 1) * P],
-                early_gain_sb[:, g, :],
-                P,
-            )
-
-        def quant_first(j, g):
-            lo = g * ROWS + j * P
-            nc.vector.quantize_mx(
-                out=q_codes[(0, EARLY)][:, lo : lo + P].bitcast(FP8X4),
-                scales=q_scales[(0, EARLY)][:, lo : lo + P],
-                in_=q_bf[(0, EARLY)][:, 4 * lo : 4 * (lo + P)],
-            )
-
-        def copy_first(j):
-            b, bank = turned[("first", j)]
-            nc.scalar.copy(
-                out=q_bf[(0, PLAIN)][:].bitcast(F32).rearrange("p (g j r u) -> p g j r u", g=PASSES, j=2, u=2)[:, :, j],
-                in_=bank[:].rearrange("p (g u r) -> p g r u", g=PASSES, u=2),
-            )
-            free_banks.append(b)
+                turned[("q", 0, g)] = take_bank()
+            for j in range(2):
+                words = first_raw[j][:].bitcast(F32)
+                for g in range(PASSES):
+                    for u in range(2):
+                        col = u * ROWS + j * P
+                        nc.tensor.transpose(
+                            turned[("q", 0, g)][1][:, col : col + P],
+                            words[:, 2 * g * P + u : 2 * (g + 1) * P : 2],
+                            ident[:],
+                        )
 
         def turn_k(c, h):
             if h == 0:
@@ -394,7 +373,8 @@ def tile_cross_layer_key_scores_s1_kernel(
 
         setup()
         load_early_gain()
-        load_q(0)
+        load_first(0)
+        load_first(1)
         load_k(0, 0)
         load_w(0)
         make_zeros()
@@ -418,8 +398,8 @@ def tile_cross_layer_key_scores_s1_kernel(
         load_k(3, 0)
         load_k(3, 1)
         load_bias(1)
-        warm_up(22)
-        turn_q(0)
+        warm_up(16)
+        turn_first()
         warm_up(10)
         turn_k(0, 0)
         for g in range(2):
@@ -427,8 +407,9 @@ def tile_cross_layer_key_scores_s1_kernel(
             copy_q(0, g)
         quant_q(0, EARLY, (0,))
         quant_q(0, EARLY, (1,))
-        sort_k(0, 1)
         sort_q(1)
+        sort_k(1, 0)
+        sort_k(1, 1)
         early(0, 0)
         early(1, 0)
         gain_k(0, 0, 0)
@@ -436,40 +417,42 @@ def tile_cross_layer_key_scores_s1_kernel(
         turn_k(0, 1)
         quant_q(0, PLAIN)
         early(0, 1)
-        turn_q(1)
+        early(1, 1)
         gain_k(0, 1, 0)
         gain_k(0, 1, 1)
-        copy_q(1, 0)
-        copy_q(1, 1)
-        early(1, 1)
-        sort_k(1, 1)
-        turn_k(1, 0)
+        turn_q(1)
         quant_k(0, 0)
         quant_k(0, 1)
-        sort_q(2)
         mid(0, 0)
         mid(1, 0)
-        gain_q(1)
-        turn_k(1, 1)
+        for g in range(2):
+            gain_q_from_psum(1, g)
+        for g in range(2):
+            copy_q(1, g)
+        turn_k(1, 0)
+        quant_q(1, EARLY)
+        early(2, 0)
+        early(3, 0)
         park(0, 0)
         park(1, 0)
-        quant_q(1, PLAIN)
-        quant_q(1, EARLY)
         gain_k(1, 0, 0)
+        quant_q(1, PLAIN)
         gain_k(1, 0, 1)
-        group(2, 0)
+        turn_k(1, 1)
         gain_k(1, 1, 0)
         gain_k(1, 1, 1)
+        mid(2, 0)
+        mid(3, 0)
+        sort_q(2)
         sort_q(3)
-        group(3, 0)
         quant_k(1, 0)
         quant_k(1, 1)
-        turn_q(2)
         finish(2, 0)
+        turn_q(2)
         turn_q(3)
         copy_q(2, 0)
         copy_q(2, 1)
-        finish(3, 0)
+        park(3, 0)
         copy_q(3, 0)
         copy_q(3, 1)
         mid(0, 1)
@@ -484,13 +467,13 @@ def tile_cross_layer_key_scores_s1_kernel(
         sort_k(2, 1)
         group(3, 1)
         gain_q(3)
-        park(2, 1)
         group(4, 0)
         quant_q(3, PLAIN)
         quant_q(3, EARLY)
+        finish(2, 1)
         park(3, 1)
-        finish_parked(2, 1, nc.gpsimd)
         finish_parked(3, 1, nc.gpsimd)
+        finish_parked(0, 0, nc.gpsimd)
         group(5, 0)
         park(4, 0)
         turn_k(2, 0)
@@ -519,26 +502,32 @@ def tile_cross_layer_key_scores_s1_kernel(
         gain_k(3, 0, 1)
         group(7, 1)
         finish(6, 1)
-        parked = [(6, 0), (0, 0), (1, 0), (0, 1), (1, 1), (4, 0), (5, 0)]
+        parked = [(6, 0), (1, 0), (3, 0), (0, 1), (1, 1), (4, 0), (5, 0)]
         extra = [
             lambda: gain_k(3, 1, 0), lambda: gain_k(3, 1, 1),
             lambda: quant_k(3, 0), lambda: quant_k(3, 1),
         ]
         finish_parked(*parked.pop(0), nc.gpsimd)
         finish_parked(*parked.pop(0), nc.gpsimd)
-        prev = (7, 1)
+        done = [(7, 1)]
         for c in (2, 3):
-            for m in range(8):
-                if (m, c) != (7, 3):
-                    group(m, c)
-                    finish(*prev)
+            for m in range(0, 8, 2):
+                pair = [m] if (m, c) == (6, 3) else [m, m + 1]
+                for x in pair:
+                    early(x, c)
+                for x in pair:
+                    if done:
+                        finish(*done.pop(0))
                     if extra:
                         extra.pop(0)()
                     if parked:
                         finish_parked(*parked.pop(0), nc.gpsimd)
-                    prev = (m, c)
+                for x in pair:
+                    mid(x, c)
+                    done.append((x, c))
         narrow_group(7, 3, 0)
-        finish(*prev)
+        for mc in done:
+            finish(*mc)
         for part in range(1, 4):
             narrow_group(7, 3, part)
             narrow_finish(7, 3, part - 1)

from contextlib import ExitStack

import concourse.mybir as mybir
from concourse.masks import make_identity

M, D, T = 1024, 1024, 2048
FLOPS = 2 * 2 * M * D * T

F32 = mybir.dt.float32
BF16 = mybir.dt.bfloat16
I32 = mybir.dt.int32
U32 = mybir.dt.uint32
U8 = mybir.dt.uint8
FP8X4 = mybir.dt.float8_e4m3fn_x4
FP4X4 = mybir.dt.float4_e2m1fn_x4
ALU = mybir.AluOpType
ACT = mybir.ActivationFunctionType

P = 128
PASSES = 2
Q_TILES = M // P
ROWS = 256
CHUNK = 512
BANK = 512
EARLY, PLAIN = 0, 1
OUT_BUFS = 20


def tile_cross_layer_key_scores_s1_kernel(
    tc, q, early_words, early_scales, early_gain, mid_keys, mid_gain, temp, key_bias, out
):
    nc = tc.nc
    q_rows = q.rearrange("(p j) k -> p j k", j=Q_TILES)
    out_rows = out.rearrange("(p j) n -> p j n", j=Q_TILES)
    w_words = early_words.bitcast(I32).rearrange("g p w -> p g w")
    w_scale_rows = early_scales.bitcast(I32)

    with ExitStack() as ctx:
        keep = ctx.enter_context(tc.tile_pool(name="keep", bufs=1))
        stage = ctx.enter_context(tc.tile_pool(name="stage", bufs=2))
        psum = ctx.enter_context(tc.psum_pool(name="psum", bufs=1))
        ctx.enter_context(tc.manual_schedule())

        def kept(name, shape, dtype):
            return keep.tile(shape, dtype, name=name, tag=name, align_bytes=256)

        ident = kept("ident", [P, P], F32)
        early_gain_sb = kept("early_gain_sb", [P, PASSES, 4], BF16)
        mid_gain_sb = kept("mid_gain_sb", [P, PASSES, 4], BF16)
        temp_bf = kept("temp_bf", [P, Q_TILES], BF16)
        temp_sb = kept("temp_sb", [P, Q_TILES], F32)
        bias_all = [kept("bias_all%d" % half, [P, T // 2], BF16) for half in range(2)]
        zero_codes = kept("zero_codes", [P, P], U32)
        zero_scales = kept("zero_scales", [P, P], U8)
        w_scales = [kept("w_scales%d" % half, [P, T], U8) for half in range(2)]

        q_raw, q_sorted, q_bf, q_codes, q_scales = {}, {}, {}, {}, {}
        k_raw, k_sorted, k_bf, k_codes, k_scales = {}, {}, {}, {}, {}
        w_codes, turned, sums, results, first_raw = {}, {}, {}, {}, {}
        free_banks = list(range(8))

        def take_bank():
            b = free_banks.pop(0)
            return b, psum.tile([P, BANK], F32, name="bank%d" % b, tag="bank%d" % b)

        def setup():
            make_identity(nc, ident[:])

        def clear_scales(half):
            nc.vector.memset(w_scales[half][:].bitcast(I32), 0)

        def make_zeros():
            zeros = kept("zeros", [P, 4 * P], BF16)
            nc.vector.memset(zeros[:], 0.0)
            nc.vector.quantize_mx(out=zero_codes[:].bitcast(FP8X4), scales=zero_scales[:], in_=zeros[:])

        def warm_up(passes):
            b, bank = take_bank()
            for n in range(passes):
                nc.tensor.matmul_mx(
                    out=bank[:, (n % 4) * P : (n % 4 + 1) * P],
                    lhsT=zero_codes[:].bitcast(FP8X4),
                    lhsT_scale=zero_scales[:],
                    rhs=zero_codes[:].bitcast(FP8X4),
                    rhs_scale=zero_scales[:],
                    start=True,
                    stop=True,
                )
            free_banks.append(b)

        def load_bias(half):
            cols = slice(half * T // 2, (half + 1) * T // 2)
            nc.sync.dma_start(out=bias_all[half][:], in_=key_bias[cols].partition_broadcast(P))

        def load_early_gain():
            nc.scalar.dma_start(out=early_gain_sb[:], in_=early_gain.rearrange("(g p t) -> p g t", g=PASSES, t=4))
            nc.scalar.dma_start(out=temp_bf[:], in_=temp.rearrange("(p j) -> p j", j=Q_TILES))

        def load_first(j):
            first_raw[j] = kept("first_raw%d" % j, [P, D], BF16)
            nc.sync.dma_start(out=first_raw[j][:], in_=q_rows[:, j, :])

        def load_mid_gain():
            nc.scalar.dma_start(out=mid_gain_sb[:], in_=mid_gain.rearrange("(g p t) -> p g t", g=PASSES, t=4))

        def load_scales(half, queue):
            plane = w_scales[half][:].bitcast(I32).rearrange("p (g w) -> p g w", g=PASSES)
            words = T // 8
            for quad in range(4):
                queue.dma_start(
                    out=plane[32 * quad : 32 * quad + 4],
                    in_=w_scale_rows[:, 4 * quad : 4 * quad + 4, half * words : (half + 1) * words].rearrange(
                        "g r w -> r g w"
                    ),
                )

        def widen_temp():
            nc.scalar.activation(out=temp_sb[:], in_=temp_bf[:], func=ACT.Copy)

        def load_q(i):
            q_raw[i] = kept("q_raw%d" % i, [P, 2 * D], BF16)
            nc.sync.dma_start(
                out=q_raw[i][:], in_=q_rows[:, 2 * i : 2 * i + 2, :].rearrange("p j k -> p (j k)")
            )

        def load_k(c, h):
            k_raw[(c, h)] = kept("k_raw%d%d" % (c, h), [P, 2 * D], BF16)
            first = c * CHUNK + h * ROWS
            nc.sync.dma_start(
                out=k_raw[(c, h)][:].rearrange("p (j k) -> p j k", j=2),
                in_=mid_keys[first : first + ROWS, :].rearrange("(j p) k -> p j k", p=P),
            )

        def load_w(c, n=1):
            words = CHUNK // 2
            tile = kept("w_codes%d" % c, [P, PASSES, n * 2 * CHUNK], U8)
            nc.sync.dma_start(out=tile[:].bitcast(I32), in_=w_words[:, :, c * words : (c + n) * words])
            for x in range(n):
                for g in range(PASSES):
                    w_codes[(c + x, g)] = tile[:, g, x * 2 * CHUNK : (x + 1) * 2 * CHUNK]

        def sort_words(raw):
            tile = stage.tile([P, D], F32, name="sorted_words", tag="sorted_words", bufs=3, align_bytes=256)
            nc.scalar.copy(
                out=tile[:].rearrange("p (a u w) -> p a u w", u=2, w=P),
                in_=raw[:].bitcast(F32).rearrange("p (a w u) -> p a u w", u=2, w=P),
            )
            return tile

        def sort_q(i):
            q_sorted[i] = sort_words(q_raw[i])

        def sort_k(c, h):
            k_sorted[(c, h)] = sort_words(k_raw[(c, h)])

        def turn(key, raw, in_order):
            for g in range(PASSES):
                b, bank = take_bank()
                turned[key + (g,)] = (b, bank)
                for u in range(2):
                    for j in range(2):
                        base = (j * PASSES + g) * 2 * P
                        if in_order is None:
                            words = raw[:].bitcast(F32)[:, base + u : base + 2 * P : 2]
                        else:
                            words = in_order[:, base + u * P : base + (u + 1) * P]
                        col = u * ROWS + j * P
                        nc.tensor.transpose(bank[:, col : col + P], words, ident[:])

        def new_q(i):
            for kind in (EARLY, PLAIN):
                q_bf[(i, kind)] = stage.tile(
                    [P, PASSES * ROWS * 4], BF16, name="q_bf%d" % kind, tag="q_bf%d" % kind, align_bytes=256
                )
                q_codes[(i, kind)] = kept("q_codes%d%d" % (i, kind), [P, PASSES * ROWS], U32)
                q_scales[(i, kind)] = kept("q_scales%d%d" % (i, kind), [P, PASSES * ROWS], U8)

        def turn_q(i):
            new_q(i)
            turn(("q", i), q_raw[i], q_sorted.get(i))

        def turn_first():
            new_q(0)
            for g in range(PASSES):
                turned[("q", 0, g)] = take_bank()
            for j in range(2):
                words = first_raw[j][:].bitcast(F32)
                for g in range(PASSES):
                    for u in range(2):
                        col = u * ROWS + j * P
                        nc.tensor.transpose(
                            turned[("q", 0, g)][1][:, col : col + P],
                            words[:, 2 * g * P + u : 2 * (g + 1) * P : 2],
                            ident[:],
                        )

        def turn_k(c, h):
            if h == 0:
                for g in range(PASSES):
                    k_bf[(c, g)] = stage.tile(
                        [P, CHUNK * 4], BF16, name="k_bf%d" % g, tag="k_bf%d" % g, align_bytes=256
                    )
                    k_codes[(c, g)] = kept("k_codes%d%d" % (c, g), [P, CHUNK], U32)
                    k_scales[(c, g)] = kept("k_scales%d%d" % (c, g), [P, CHUNK], U8)
            turn(("k", c, h), k_raw[(c, h)], k_sorted.get((c, h)))

        def gain_from_psum(target, words, gain, rows):
            nc.vector.tensor_tensor(
                out=target.rearrange("p (r u e) -> p r u e", u=2, e=2),
                in0=words.bitcast(BF16).rearrange("p (u r e) -> p r u e", u=2, e=2),
                in1=gain.rearrange("p (u e) -> p u e", u=2).unsqueeze(1).to_broadcast([P, rows, 2, 2]),
                op=ALU.mult,
            )

        def gain_q_from_psum(i, g):
            width = ROWS * 4
            gain_from_psum(
                q_bf[(i, EARLY)][:, g * width : (g + 1) * width],
                turned[("q", i, g)][1][:],
                early_gain_sb[:, g, :],
                ROWS,
            )

        def copy_q(i, g):
            b, bank = turned[("q", i, g)]
            width = ROWS * 2
            nc.scalar.copy(
                out=q_bf[(i, PLAIN)][:].bitcast(F32)[:, g * width : (g + 1) * width].rearrange(
                    "p (r u) -> p r u", u=2
                ),
                in_=bank[:].rearrange("p (u r) -> p r u", u=2),
            )
            free_banks.append(b)

        def gain_q(i):
            nc.vector.tensor_tensor(
                out=q_bf[(i, EARLY)][:].rearrange("p (g r t) -> p g r t", g=PASSES, t=4),
                in0=q_bf[(i, PLAIN)][:].rearrange("p (g r t) -> p g r t", g=PASSES, t=4),
                in1=early_gain_sb[:].unsqueeze(2).to_broadcast([P, PASSES, ROWS, 4]),
                op=ALU.mult,
            )

        def quant_q(i, kind, gs=(0, 1)):
            lo, hi = gs[0] * ROWS, (gs[-1] + 1) * ROWS
            nc.vector.quantize_mx(
                out=q_codes[(i, kind)][:, lo:hi].bitcast(FP8X4),
                scales=q_scales[(i, kind)][:, lo:hi],
                in_=q_bf[(i, kind)][:, 4 * lo : 4 * hi],
            )

        def gain_k(c, h, g):
            b, bank = turned[("k", c, h, g)]
            width = ROWS * 4
            gain_from_psum(k_bf[(c, g)][:, h * width : (h + 1) * width], bank[:], mid_gain_sb[:, g, :], ROWS)
            free_banks.append(b)

        def quant_k(c, g):
            nc.vector.quantize_mx(
                out=k_codes[(c, g)][:].bitcast(FP8X4), scales=k_scales[(c, g)][:], in_=k_bf[(c, g)][:]
            )

        def q_operand(m, kind, g):
            cols = slice(g * ROWS + (m % 2) * P, g * ROWS + (m % 2 + 1) * P)
            return q_codes[(m // 2, kind)][:, cols].bitcast(FP8X4), q_scales[(m // 2, kind)][:, cols]

        def early(m, c):
            sums[(m, c)] = take_bank()
            for g in range(PASSES):
                codes, scales = q_operand(m, EARLY, g)
                nc.tensor.matmul_mx(
                    out=sums[(m, c)][1][:],
                    lhsT=codes,
                    lhsT_scale=scales,
                    rhs=w_codes[(c, g)].bitcast(FP4X4),
                    rhs_scale=w_scales[c // 2][:, (2 * g + c % 2) * CHUNK : (2 * g + c % 2 + 1) * CHUNK],
                    start=(g == 0),
                    stop=False,
                )

        def mid(m, c):
            for g in range(PASSES):
                codes, scales = q_operand(m, PLAIN, g)
                nc.tensor.matmul_mx(
                    out=sums[(m, c)][1][:],
                    lhsT=codes,
                    lhsT_scale=scales,
                    rhs=k_codes[(c, g)][:].bitcast(FP8X4),
                    rhs_scale=k_scales[(c, g)][:],
                    start=False,
                    stop=(g == PASSES - 1),
                )

        def group(m, c):
            early(m, c)
            mid(m, c)

        def narrow_group(m, c, part):
            b, bank = take_bank()
            sums[(m, c, part)] = (b, bank)
            lo = part * P
            for g in range(PASSES):
                codes, scales = q_operand(m, EARLY, g)
                base = (2 * g + c % 2) * CHUNK + lo
                nc.tensor.matmul_mx(
                    out=bank[:, :P],
                    lhsT=codes,
                    lhsT_scale=scales,
                    rhs=w_codes[(c, g)][:, 2 * lo : 2 * (lo + P)].bitcast(FP4X4),
                    rhs_scale=w_scales[c // 2][:, base : base + P],
                    start=(g == 0),
                    stop=False,
                )
            for g in range(PASSES):
                codes, scales = q_operand(m, PLAIN, g)
                nc.tensor.matmul_mx(
                    out=bank[:, :P],
                    lhsT=codes,
                    lhsT_scale=scales,
                    rhs=k_codes[(c, g)][:, lo : lo + P].bitcast(FP8X4),
                    rhs_scale=k_scales[(c, g)][:, lo : lo + P],
                    start=False,
                    stop=(g == PASSES - 1),
                )

        def narrow_finish(m, c, part):
            b, bank = sums[(m, c, part)]
            if part % 2 == 0:
                results[(m, c)] = stage.tile([P, 2 * P], F32, name="narrow_result", tag="narrow_result")
            first = c * CHUNK + part * P
            nc.vector.scalar_tensor_tensor(
                out=results[(m, c)][:, (part % 2) * P : (part % 2 + 1) * P],
                in0=bank[:, :P],
                scalar=temp_sb[:, m : m + 1],
                in1=bias_all[c // 2][:, first % (T // 2) : first % (T // 2) + P],
                op0=ALU.mult,
                op1=ALU.add,
            )
            free_banks.append(b)
            if part % 2 == 1:
                nc.sync.dma_start(out=out_rows[:, m, first - P : first + P], in_=results[(m, c)][:])

        def new_result(m, c):
            results[(m, c)] = stage.tile([P, CHUNK], F32, name="result", tag="result", bufs=OUT_BUFS)
            return results[(m, c)]

        def store(m, c):
            nc.sync.dma_start(out=out_rows[:, m, c * CHUNK : (c + 1) * CHUNK], in_=results[(m, c)][:])

        def finish(m, c):
            b, bank = sums[(m, c)]
            nc.vector.scalar_tensor_tensor(
                out=new_result(m, c)[:],
                in0=bank[:],
                scalar=temp_sb[:, m : m + 1],
                in1=bias_all[c // 2][:, (c % 2) * CHUNK : (c % 2 + 1) * CHUNK],
                op0=ALU.mult,
                op1=ALU.add,
            )
            free_banks.append(b)
            store(m, c)

        def park(m, c):
            b, bank = sums[(m, c)]
            nc.scalar.activation(out=new_result(m, c)[:], in_=bank[:], func=ACT.Copy, scale=temp_sb[:, m : m + 1])
            free_banks.append(b)

        def finish_parked(m, c, engine):
            result = results[(m, c)]
            engine.tensor_tensor(
                out=result[:], in0=result[:], in1=bias_all[c // 2][:, (c % 2) * CHUNK : (c % 2 + 1) * CHUNK], op=ALU.add
            )
            store(m, c)

        setup()
        load_early_gain()
        load_first(0)
        load_first(1)
        load_k(0, 0)
        load_w(0)
        make_zeros()
        clear_scales(0)
        load_scales(0, nc.scalar)
        clear_scales(1)
        load_mid_gain()
        widen_temp()
        load_k(0, 1)
        load_w(1)
        load_q(1)
        load_k(1, 0)
        load_k(1, 1)
        load_q(2)
        load_q(3)
        load_bias(0)
        load_k(2, 0)
        load_k(2, 1)
        load_w(2, 2)
        load_scales(1, nc.sync)
        load_k(3, 0)
        load_k(3, 1)
        load_bias(1)
        warm_up(16)
        turn_first()
        warm_up(10)
        turn_k(0, 0)
        for g in range(2):
            gain_q_from_psum(0, g)
            copy_q(0, g)
        quant_q(0, EARLY, (0,))
        quant_q(0, EARLY, (1,))
        sort_q(1)
        sort_k(1, 0)
        sort_k(1, 1)
        early(0, 0)
        early(1, 0)
        gain_k(0, 0, 0)
        gain_k(0, 0, 1)
        turn_k(0, 1)
        quant_q(0, PLAIN)
        early(0, 1)
        early(1, 1)
        gain_k(0, 1, 0)
        gain_k(0, 1, 1)
        turn_q(1)
        quant_k(0, 0)
        quant_k(0, 1)
        mid(0, 0)
        mid(1, 0)
        for g in range(2):
            gain_q_from_psum(1, g)
        for g in range(2):
            copy_q(1, g)
        turn_k(1, 0)
        quant_q(1, EARLY)
        early(2, 0)
        early(3, 0)
        park(0, 0)
        park(1, 0)
        gain_k(1, 0, 0)
        quant_q(1, PLAIN)
        gain_k(1, 0, 1)
        turn_k(1, 1)
        gain_k(1, 1, 0)
        gain_k(1, 1, 1)
        mid(2, 0)
        mid(3, 0)
        sort_q(2)
        sort_q(3)
        quant_k(1, 0)
        quant_k(1, 1)
        finish(2, 0)
        turn_q(2)
        turn_q(3)
        copy_q(2, 0)
        copy_q(2, 1)
        park(3, 0)
        copy_q(3, 0)
        copy_q(3, 1)
        mid(0, 1)
        mid(1, 1)
        gain_q(2)
        group(2, 1)
        quant_q(2, PLAIN)
        quant_q(2, EARLY)
        park(0, 1)
        park(1, 1)
        sort_k(2, 0)
        sort_k(2, 1)
        group(3, 1)
        gain_q(3)
        group(4, 0)
        quant_q(3, PLAIN)
        quant_q(3, EARLY)
        finish(2, 1)
        park(3, 1)
        finish_parked(3, 1, nc.gpsimd)
        finish_parked(0, 0, nc.gpsimd)
        group(5, 0)
        park(4, 0)
        turn_k(2, 0)
        turn_k(2, 1)
        park(5, 0)
        group(4, 1)
        gain_k(2, 0, 0)
        gain_k(2, 0, 1)
        gain_k(2, 1, 0)
        gain_k(2, 1, 1)
        group(5, 1)
        sort_k(3, 0)
        sort_k(3, 1)
        finish(4, 1)
        group(6, 0)
        quant_k(2, 0)
        quant_k(2, 1)
        finish(5, 1)
        group(7, 0)
        park(6, 0)
        turn_k(3, 0)
        turn_k(3, 1)
        finish(7, 0)
        group(6, 1)
        gain_k(3, 0, 0)
        gain_k(3, 0, 1)
        group(7, 1)
        finish(6, 1)
        parked = [(6, 0), (1, 0), (3, 0), (0, 1), (1, 1), (4, 0), (5, 0)]
        extra = [
            lambda: gain_k(3, 1, 0), lambda: gain_k(3, 1, 1),
            lambda: quant_k(3, 0), lambda: quant_k(3, 1),
        ]
        finish_parked(*parked.pop(0), nc.gpsimd)
        finish_parked(*parked.pop(0), nc.gpsimd)
        done = [(7, 1)]
        for c in (2, 3):
            for m in range(0, 8, 2):
                pair = [m] if (m, c) == (6, 3) else [m, m + 1]
                for x in pair:
                    early(x, c)
                for x in pair:
                    if done:
                        finish(*done.pop(0))
                    if extra:
                        extra.pop(0)()
                    if parked:
                        finish_parked(*parked.pop(0), nc.gpsimd)
                for x in pair:
                    mid(x, c)
                    done.append((x, c))
        narrow_group(7, 3, 0)
        for mc in done:
            finish(*mc)
        for part in range(1, 4):
            narrow_group(7, 3, part)
            narrow_finish(7, 3, part - 1)
        narrow_finish(7, 3, 3)
